import numpy as np, ml_dtypes
CORES = [1,129,9,137,57,185,105,233,113,241,121,249]
N = 12
R, T = 4096, 256
CAPP = 64
def entries(a): return a.T.reshape(-1)
def pack(v, P): return np.ascontiguousarray(np.asarray(v, np.int32).reshape(-1, P).T)
def lists(rng, how):
    I = rng.integers(0, N * R, (N, T))
    O = np.stack([rng.permutation(np.repeat(np.arange(N), CAPP))[:T] for r in range(N)])
    if how == "full": O = np.stack([rng.permutation(np.repeat(rng.permutation(N)[:T // CAPP], CAPP)) for r in range(N)])
    I = R * O + rng.integers(0, R, (N, T))
    if how == "alike": I = R * O + rng.integers(0, R, (N, 1))
    if how == "edge": I = R * O + np.where(rng.random((N, T)) < 0.5, 0, R - 1)
    if how == "sorted": I = np.sort(I, axis=1)
    return {"idx": np.stack([pack(I[r], 16) for r in range(N)])}
def setup_inputs(rng):
    return dict({"x": rng.standard_normal((N, 128, T), dtype=np.float32).astype(ml_dtypes.bfloat16), "tab": rng.standard_normal((N, 128, R), dtype=np.float32).astype(ml_dtypes.bfloat16)}, **lists(rng, "uniform"))
def setup_inputs_alike(rng):
    d = setup_inputs(rng); d.update(lists(rng, "alike"))
    for k in ("x", "tab"): d[k] = (d[k].astype(np.float32) * 1024.0).astype(d[k].dtype)
    return d
def setup_inputs_edge(rng):
    d = setup_inputs(rng); d.update(lists(rng, "edge"))
    for k in ("x", "tab"): d[k] = (d[k].astype(np.float32) * (1 / 1024.0)).astype(d[k].dtype)
    return d
def setup_inputs_full(rng):
    d = setup_inputs(rng); d.update(lists(rng, "full"))
    return d
def setup_inputs_sorted(rng):
    d = setup_inputs(rng); d.update(lists(rng, "sorted"))
    return d
def check_inputs(x):
    bad = []
    if x["idx"].min() < 0 or x["idx"].max() >= N * R: bad.append("idx out of range")
    if max(int(np.bincount(entries(a) // R, minlength=N).max()) for a in x["idx"]) > CAPP: bad.append("more than CAPP entries of a list point into one rank's part")
    return bad
def reference(x, tab, idx):
    A = np.concatenate(list(tab), axis=1).astype(np.float64)
    return {"y": np.stack([x[r].astype(np.float64) + A[:, entries(idx[r])] for r in range(N)]).astype(ml_dtypes.bfloat16)}

@@ -1,0 +1,244 @@
+import numpy as np
+from concourse.bass import DstId, RemoteDMATransfer
+from concourse.mybir import dt, AluOpType, AxisListType, ActivationFunctionType
+
+N = 12
+RP = 4096
+TT = 256
+CAP = 64
+NSIM = 256
+GRP = 2
+
+SCRATCH = {
+    "idxs": ("sbuf", [128, 2], "int32"),
+    "tabs": ("sbuf", [128, RP], "bfloat16"),
+    "xs": ("sbuf", [128, TT], "bfloat16"),
+    "ys": ("sbuf", [128, TT], "bfloat16"),
+    "rowj": ("sbuf", [128, 128], "float32"),
+    "i16": ("sbuf", [128, 128], "float32"),
+    "pci": ("sbuf", [128, 1], "int32"),
+    "pcf": ("sbuf", [128, 1], "float32"),
+    "ones": ("sbuf", [128, 128], "bfloat16"),
+    "ltri": ("sbuf", [128, 128], "bfloat16"),
+    "ib": ("sbuf", [128, 4], "int32"),
+    "fb": ("sbuf", [128, 4], "float32"),
+    "eh": ("sbuf", [128, 32], "bfloat16"),
+    "o64": ("sbuf", [128, 2], "float32"),
+    "ec": ("sbuf", [128, 32], "float32"),
+    "kk": ("sbuf", [128, 2], "float32"),
+    "posi": ("sbuf", [128, 2], "int32"),
+    "kb": ("sbuf", [128, 4], "int32"),
+    "kf": ("sbuf", [128, 4], "float32"),
+    "a0": ("sbuf", [128, 128], "float32"),
+    "a1": ("sbuf", [128, 128], "float32"),
+    "bb": ("sbuf", [128, 96], "float32"),
+    "req": ("sbuf", [128, 4 * N], "uint16"),
+    "posf": ("sbuf", [128, 2], "float32"),
+    "pb": ("sbuf", [128, 2], "int32"),
+    "pbf": ("sbuf", [128, 2], "float32"),
+    "pm": ("sbuf", [128, 128], "float32"),
+    "cc": ("sbuf", [128, 2], "float32"),
+    "cm": ("sbuf", [128, 32], "float32"),
+    "a2": ("sbuf", [128, 128], "float32"),
+    "a3": ("sbuf", [128, 128], "float32"),
+    "fo": ("sbuf", [128, 16], "uint16"),
+    "offs": ("sbuf", [128, 4 * N], "uint16"),
+    "offx": ("sbuf", [128, 4 * N], "uint16"),
+    "gs": ("sbuf", [128, CAP * N], "bfloat16"),
+    "gx": ("sbuf", [128, CAP * N], "bfloat16"),
+    "land": ("sbuf", [128, CAP * N], "bfloat16"),
+    "rq": ("sbuf", [128, 4 * N], "uint16"),
+    "rl": ("sbuf", [128, CAP * GRP], "bfloat16"),
+    "ps1": ("psum", [128, 512], "float32"),
+    "ps2": ("psum", [128, 512], "float32"),
+    "ps3": ("psum", [128, 512], "float32"),
+}
+SEMAPHORES = ["sidx", "stab", "sx", "sy", "gi", "v", "p", "a", "ls", "fq", "fr", "rqs", "rqx", "lnd"]
+
+_memo = {}
+
+
+def _engines(mask):
+    return [e for e in range(16) if (mask >> e) & 1]
+
+
+def _calls(items, engs):
+    out, i = [], 0
+    while i < len(items):
+        t = 1
+        while t * 2 <= min(len(items) - i, len(engs)):
+            t *= 2
+        w = len(engs) // t
+        out.append([(sum(1 << e for e in engs[j * w:(j + 1) * w]),) + tuple(items[i + j]) for j in range(t)])
+        i += t
+    return out
+
+
+def plan(cores, topo):
+    if "p" in _memo:
+        return _memo["p"]
+    n = len(cores)
+    same, cross, relays, groups = [], [], [], []
+    for r, c in enumerate(cores):
+        ring = [(r + 1 + i) % n for i in range(n - 1)]
+        same.append([s for s in ring if topo.same_plane(c, cores[s])])
+        cross.append([s for s in ring if not topo.same_plane(c, cores[s])])
+        cand = [d for d in range(NSIM) if d not in cores and topo.host(d) == topo.host(c) and topo.chip(d) == topo.chip(c)
+                and all(topo.may_write(d, cores[s]) for s in cross[r])]
+        cand.sort(key=lambda d: (topo.die(d) != topo.die(c), d))
+        k = min(len(cand), (len(cross[r]) + GRP - 1) // GRP)
+        relays.append(cand[:k])
+        groups.append([cross[r][i * GRP:(i + 1) * GRP] for i in range(k)])
+    sends, expect, local, role = {}, {}, {}, {}
+
+    def add(core, phase, items, engs):
+        cs = _calls(items, engs)
+        sends.setdefault(core, {})[phase] = cs
+        for call in cs:
+            for (mask, d, sem, s, t) in call:
+                e = len(_engines(mask))
+                expect[(d, sem)] = expect.get((d, sem), 0) + e
+                local[core] = local.get(core, 0) + e
+
+    for r, c in enumerate(cores):
+        off = _engines(topo.mask(c, cores[same[r][0]]))
+        onc = _engines(topo.mask(c, relays[r][0]))
+        rest = [e for e in onc if e not in off]
+        add(c, "qfeed", [(d, "fq", ("req", 0, 4 * n), ("rq", 0, 4 * n)) for d in relays[r]], onc)
+        add(c, "qdir", [(cores[s], "rqs", ("req", 4 * s, 4 * s + 4), ("offs", 4 * same[s].index(r), 4 * same[s].index(r) + 4))
+                        for s in same[r]], off)
+        add(c, "rdir", [(cores[s], "lnd", ("gs", CAP * i, CAP * i + CAP), ("land", CAP * r, CAP * r + CAP))
+                        for i, s in enumerate(same[r])], off)
+        add(c, "rfeed", [(d, "fr", ("gx", CAP * GRP * i, CAP * GRP * (i + 1)), ("rl", 0, CAP * GRP))
+                         for i, d in enumerate(relays[r])], onc if len(same[r]) < len(cross[r]) else rest)
+        for i, d in enumerate(relays[r]):
+            role[d] = r
+            eo = _engines(topo.mask(d, cores[groups[r][i][0]]))
+            add(d, "q", [(cores[s], "rqx", ("rq", 4 * s, 4 * s + 4), ("offx", 4 * cross[s].index(r), 4 * cross[s].index(r) + 4))
+                         for s in groups[r][i]], eo)
+            add(d, "r", [(cores[s], "lnd", ("rl", CAP * j, CAP * j + CAP), ("land", CAP * r, CAP * r + CAP))
+                         for j, s in enumerate(groups[r][i])], eo)
+    _memo["p"] = dict(same=same, cross=cross, sends=sends, expect=expect, local=local, role=role)
+    return _memo["p"]
+
+
+def _emit(g, T, topo, core, calls):
+    for call in calls:
+        trs = []
+        for (mask, d, sem, s, t) in call:
+            rid, pid = topo.addr(d, core)
+            trs.append(RemoteDMATransfer(dst_ids=[DstId(rid=rid, pnc=pid)], dma_engine_mask=mask, remote_sem=T.sem[sem],
+                                         src=T[s[0]][:, s[1]:s[2]], dst=T[t[0]][:, t[1]:t[2]]))
+        g.remote_dma_fused(trs, local_sem=T.sem.ls)
+
+
+def rank_program(g, core, T, topo):
+    P = plan(list(T.cores), topo)
+    rank = T.rank_of(core)
+    S = T.sem
+    if rank is None:
+        if core not in P["role"]:
+            return
+        g.wait_ge(S.fq, P["expect"][(core, "fq")])
+        _emit(g, T, topo, core, P["sends"][core]["q"])
+        g.wait_ge(S.fr, P["expect"][(core, "fr")])
+        _emit(g, T, topo, core, P["sends"][core]["r"])
+        g.wait_ge(S.ls, P["local"][core])
+        return
+
+    A = AluOpType
+    ns, nx = len(P["same"][rank]), len(P["cross"][rank])
+    snd = P["sends"][core]
+    nv = [0]
+    vec = g.vector
+
+    def V(ins):
+        ins.then_inc(S.v, 1)
+        nv[0] += 1
+        vec.wait_ge(S.v, nv[0])
+        return nv[0]
+
+    g.sync.dma_start(T.idxs[:, :], T.idx[:, :]).then_inc(S.sidx, 16)
+    g.sync.dma_start(T.tabs[:, :], T.tab[:, :]).then_inc(S.stab, 16)
+    g.sync.dma_start(T.xs[:, :], T.x[:, :]).then_inc(S.sx, 16)
+
+    g.iota(T.rowj[:, :], [[1, 128]], 0, 0, allow_small_or_imprecise_dtypes=True).then_inc(S.gi, 1)
+    g.iota(T.pci[:, :], [[0, 1]], 0, 1).then_inc(S.gi, 1)
+    g.iota(T.i16[:, :], [[0, 8], [1, 16]], 0, 0, allow_small_or_imprecise_dtypes=True).then_inc(S.gi, 1)
+    V(vec.memset(T.ones[:, :], 1.0))
+    vec.wait_ge(S.gi, 3)
+    V(vec.tensor_copy(T.pcf[:, :], T.pci[:, :]))
+    V(vec.tensor_scalar(T.ltri[:, :], T.rowj[:, :], T.pcf[:, 0:1], None, A.is_gt))
+
+    vec.wait_ge(S.sidx, 16)
+    V(vec.tensor_scalar(T.ib[:, 0:2], T.idxs[:, :], 12, None, A.arith_shift_right))
+    V(vec.tensor_scalar(T.ib[:, 2:4], T.idxs[:, :], RP - 1, None, A.bitwise_and))
+    V(vec.tensor_copy(T.fb[:, :], T.ib[:, :]))
+    V(vec.tensor_scalar(T.eh[:, 0:16], T.rowj[:, 0:16], T.fb[:, 0:1], None, A.is_equal))
+    e_done = V(vec.tensor_scalar(T.eh[:, 16:32], T.rowj[:, 0:16], T.fb[:, 1:2], None, A.is_equal))
+    g.tensor.wait_ge(S.v, e_done)
+    g.tensor.matmul(T.ps1[:, 0:16], T.ltri[:, :], T.eh[:, 0:16], True, True).then_inc(S.p, 1)
+    g.tensor.matmul(T.ps1[:, 16:32], T.ones[:, :], T.eh[:, 0:16], True, False)
+    g.tensor.matmul(T.ps1[:, 16:32], T.ltri[:, :], T.eh[:, 16:32], False, True).then_inc(S.p, 1)
+    V(vec.tensor_scalar(T.o64[:, :], T.fb[:, 0:2], float(CAP), None, A.mult))
+    vec.wait_ge(S.p, 2)
+    V(vec.tensor_tensor(T.ec[:, :], T.eh[:, :], T.ps1[:, 0:32], A.mult))
+    V(vec.tensor_reduce(T.kk[:, 0:1], T.ec[:, 0:16], AxisListType.X, A.add))
+    V(vec.tensor_reduce(T.kk[:, 1:2], T.ec[:, 16:32], AxisListType.X, A.add))
+    V(vec.tensor_tensor(T.posi[:, :], T.kk[:, :], T.o64[:, :], A.add))
+    V(vec.tensor_scalar(T.kb[:, 0:2], T.posi[:, :], 4, None, A.arith_shift_right))
+    V(vec.tensor_scalar(T.kb[:, 2:4], T.posi[:, :], 15, None, A.bitwise_and))
+    V(vec.tensor_copy(T.kf[:, :], T.kb[:, :]))
+    V(vec.tensor_scalar(T.a0[:, :], T.i16[:, :], T.kf[:, 2:3], T.fb[:, 2:3], A.is_equal, A.mult))
+    h0 = V(vec.tensor_scalar(T.bb[:, 0:48], T.rowj[:, 0:48], T.kf[:, 0:1], None, A.is_equal))
+    g.tensor.wait_ge(S.v, h0)
+    g.tensor.matmul(T.ps2[:, 0:48], T.a0[:, :], T.bb[:, 0:48], True, False)
+    V(vec.tensor_scalar(T.a1[:, :], T.i16[:, :], T.kf[:, 3:4], T.fb[:, 3:4], A.is_equal, A.mult))
+    h1 = V(vec.tensor_scalar(T.bb[:, 48:96], T.rowj[:, 0:48], T.kf[:, 1:2], None, A.is_equal))
+    g.tensor.wait_ge(S.v, h1)
+    g.tensor.matmul(T.ps2[:, 0:48], T.a1[:, :], T.bb[:, 48:96], False, True).then_inc(S.p, 1)
+    vec.wait_ge(S.p, 3)
+    req_done = V(vec.tensor_copy(T.req[:, :], T.ps2[:, 0:48]))
+
+    g.wait_ge(S.v, req_done)
+    _emit(g, T, topo, core, snd["qfeed"])
+    _emit(g, T, topo, core, snd["qdir"])
+
+    V(vec.tensor_tensor(T.posf[:, :], T.kk[:, :], T.o64[:, :], A.add))
+    V(vec.tensor_scalar(T.pb[:, 0:1], T.pci[:, :], 3, None, A.arith_shift_right))
+    V(vec.tensor_scalar(T.pb[:, 1:2], T.pci[:, :], 7, None, A.bitwise_and))
+    V(vec.tensor_copy(T.pbf[:, :], T.pb[:, :]))
+    V(vec.tensor_scalar(T.pm[:, :], T.i16[:, :], T.pbf[:, 0:1], None, A.is_equal))
+    for h in range(2):
+        V(vec.tensor_scalar(T.cc[:, h:h + 1], T.pbf[:, 1:2], 2.0, float(h), A.mult, A.add))
+    for h in range(2):
+        V(vec.tensor_scalar(T.cm[:, 16 * h:16 * h + 16], T.rowj[:, 0:16], T.cc[:, h:h + 1], None, A.is_equal))
+    V(vec.tensor_scalar(T.a2[:, :], T.pm[:, :], T.posf[:, 0:1], None, A.mult))
+    f1 = V(vec.tensor_scalar(T.a3[:, :], T.pm[:, :], T.posf[:, 1:2], None, A.mult))
+    g.tensor.wait_ge(S.v, f1)
+    g.tensor.matmul(T.ps3[:, 0:16], T.a2[:, :], T.cm[:, 0:16], True, False)
+    g.tensor.matmul(T.ps3[:, 0:16], T.a3[:, :], T.cm[:, 16:32], False, True).then_inc(S.p, 1)
+    vec.wait_ge(S.p, 4)
+    V(vec.tensor_copy(T.fo[:, :], T.ps3[:, 0:16]))
+
+    g.scalar.wait_ge(S.stab, 16)
+    g.scalar.wait_ge(S.rqs, P["expect"][(core, "rqs")])
+    g.scalar.activation(T.gs[:, 0:CAP * ns], T.tabs[:, :].indirect(T.offs[:, 0:4 * ns]),
+                        ActivationFunctionType.Copy).then_inc(S.a, 1)
+    vec.wait_ge(S.stab, 16)
+    V(vec.tensor_copy(T.land[:, CAP * rank:CAP * rank + CAP], T.tabs[:, :].indirect(T.req[:, 4 * rank:4 * rank + 4])))
+    vec.wait_ge(S.rqx, P["expect"][(core, "rqx")])
+    gx_done = V(vec.tensor_copy(T.gx[:, 0:CAP * nx], T.tabs[:, :].indirect(T.offx[:, 0:4 * nx])))
+
+    g.wait_ge(S.a, 1)
+    _emit(g, T, topo, core, snd["rdir"])
+    g.wait_ge(S.v, gx_done)
+    _emit(g, T, topo, core, snd["rfeed"])
+
+    vec.wait_ge(S.sx, 16)
+    vec.wait_ge(S.lnd, P["expect"][(core, "lnd")])
+    y_done = V(vec.tensor_tensor(T.ys[:, :], T.land[:, :].indirect(T.fo[:, :]), T.xs[:, :], A.add))
+    g.sync.wait_ge(S.v, y_done)
+    g.sync.dma_start(T.y[:, :], T.ys[:, :]).then_inc(S.sy, 16)
+    g.sync.wait_ge(S.sy, 16)
+    g.wait_ge(S.ls, P["local"][core])

@@ -14,14 +14,14 @@ SCRATCH = {
     "tabs": ("sbuf", [128, RP], "bfloat16"),
     "xs": ("sbuf", [128, TT], "bfloat16"),
     "ys": ("sbuf", [128, TT], "bfloat16"),
-    "rowj": ("sbuf", [128, 128], "float32"),
-    "i16": ("sbuf", [128, 128], "float32"),
+    "rowj": ("sbuf", [128, 128], "bfloat16"),
+    "i16": ("sbuf", [128, 128], "bfloat16"),
     "pci": ("sbuf", [128, 1], "int32"),
     "pcf": ("sbuf", [128, 1], "float32"),
     "ones": ("sbuf", [128, 128], "bfloat16"),
     "ltri": ("sbuf", [128, 128], "bfloat16"),
-    "ib": ("sbuf", [128, 4], "int32"),
-    "fb": ("sbuf", [128, 4], "float32"),
+    "ib": ("sbuf", [128, 6], "int32"),
+    "fb": ("sbuf", [128, 6], "float32"),
     "eh": ("sbuf", [128, 32], "bfloat16"),
     "o64": ("sbuf", [128, 2], "float32"),
     "ec": ("sbuf", [128, 32], "float32"),
@@ -29,9 +29,9 @@ SCRATCH = {
     "posi": ("sbuf", [128, 2], "int32"),
     "kb": ("sbuf", [128, 4], "int32"),
     "kf": ("sbuf", [128, 4], "float32"),
-    "a0": ("sbuf", [128, 128], "float32"),
-    "a1": ("sbuf", [128, 128], "float32"),
-    "bb": ("sbuf", [128, 96], "float32"),
+    "a0": ("sbuf", [128, 128], "bfloat16"),
+    "a1": ("sbuf", [128, 128], "bfloat16"),
+    "bb": ("sbuf", [128, 192], "bfloat16"),
     "req": ("sbuf", [128, 4 * N], "uint16"),
     "posf": ("sbuf", [128, 2], "float32"),
     "pb": ("sbuf", [128, 2], "int32"),
@@ -147,14 +147,18 @@ def rank_program(g, core, T, topo):
         return
 
     A = AluOpType
+    Copy = ActivationFunctionType.Copy
     ns, nx = len(P["same"][rank]), len(P["cross"][rank])
     snd = P["sends"][core]
     nv = [0]
     vec = g.vector
+    ts = vec.tensor_scalar
 
     def V(ins):
         ins.then_inc(S.v, 1)
         nv[0] += 1
+
+    def level():
         vec.wait_ge(S.v, nv[0])
         return nv[0]
 
@@ -168,77 +172,96 @@ def rank_program(g, core, T, topo):
     V(vec.memset(T.ones[:, :], 1.0))
     vec.wait_ge(S.gi, 3)
     V(vec.tensor_copy(T.pcf[:, :], T.pci[:, :]))
-    V(vec.tensor_scalar(T.ltri[:, :], T.rowj[:, :], T.pcf[:, 0:1], None, A.is_gt))
+    level()
+    V(ts(T.ltri[:, :], T.rowj[:, :], T.pcf[:, 0:1], None, A.is_gt))
+    level()
 
     vec.wait_ge(S.sidx, 16)
-    V(vec.tensor_scalar(T.ib[:, 0:2], T.idxs[:, :], 12, None, A.arith_shift_right))
-    V(vec.tensor_scalar(T.ib[:, 2:4], T.idxs[:, :], RP - 1, None, A.bitwise_and))
+    V(ts(T.ib[:, 0:2], T.idxs[:, :], 12, None, A.arith_shift_right))
+    V(ts(T.ib[:, 2:4], T.idxs[:, :], RP - CAP, None, A.bitwise_and))
+    V(ts(T.ib[:, 4:6], T.idxs[:, :], CAP - 1, None, A.bitwise_and))
+    level()
     V(vec.tensor_copy(T.fb[:, :], T.ib[:, :]))
-    V(vec.tensor_scalar(T.eh[:, 0:16], T.rowj[:, 0:16], T.fb[:, 0:1], None, A.is_equal))
-    e_done = V(vec.tensor_scalar(T.eh[:, 16:32], T.rowj[:, 0:16], T.fb[:, 1:2], None, A.is_equal))
-    g.tensor.wait_ge(S.v, e_done)
+    level()
+    V(ts(T.eh[:, 0:16], T.rowj[:, 0:16], T.fb[:, 0:1], None, A.is_equal))
+    V(ts(T.eh[:, 16:32], T.rowj[:, 0:16], T.fb[:, 1:2], None, A.is_equal))
+    V(ts(T.o64[:, :], T.fb[:, 0:2], float(CAP), None, A.mult))
+    g.tensor.wait_ge(S.v, level())
     g.tensor.matmul(T.ps1[:, 0:16], T.ltri[:, :], T.eh[:, 0:16], True, True).then_inc(S.p, 1)
     g.tensor.matmul(T.ps1[:, 16:32], T.ones[:, :], T.eh[:, 0:16], True, False)
     g.tensor.matmul(T.ps1[:, 16:32], T.ltri[:, :], T.eh[:, 16:32], False, True).then_inc(S.p, 1)
-    V(vec.tensor_scalar(T.o64[:, :], T.fb[:, 0:2], float(CAP), None, A.mult))
     vec.wait_ge(S.p, 2)
     V(vec.tensor_tensor(T.ec[:, :], T.eh[:, :], T.ps1[:, 0:32], A.mult))
+    level()
     V(vec.tensor_reduce(T.kk[:, 0:1], T.ec[:, 0:16], AxisListType.X, A.add))
     V(vec.tensor_reduce(T.kk[:, 1:2], T.ec[:, 16:32], AxisListType.X, A.add))
+    level()
     V(vec.tensor_tensor(T.posi[:, :], T.kk[:, :], T.o64[:, :], A.add))
-    V(vec.tensor_scalar(T.kb[:, 0:2], T.posi[:, :], 4, None, A.arith_shift_right))
-    V(vec.tensor_scalar(T.kb[:, 2:4], T.posi[:, :], 15, None, A.bitwise_and))
+    V(vec.tensor_tensor(T.posf[:, :], T.kk[:, :], T.o64[:, :], A.add))
+    level()
+    V(ts(T.kb[:, 0:2], T.posi[:, :], 4, None, A.arith_shift_right))
+    V(ts(T.kb[:, 2:4], T.posi[:, :], 15, None, A.bitwise_and))
+    level()
     V(vec.tensor_copy(T.kf[:, :], T.kb[:, :]))
-    V(vec.tensor_scalar(T.a0[:, :], T.i16[:, :], T.kf[:, 2:3], T.fb[:, 2:3], A.is_equal, A.mult))
-    h0 = V(vec.tensor_scalar(T.bb[:, 0:48], T.rowj[:, 0:48], T.kf[:, 0:1], None, A.is_equal))
-    g.tensor.wait_ge(S.v, h0)
+    level()
+    for h, ah in enumerate((T.a0, T.a1)):
+        V(ts(ah[:, :], T.i16[:, :], T.kf[:, 2 + h:3 + h], None, A.is_equal))
+        V(ts(T.bb[:, 96 * h:96 * h + 48], T.rowj[:, 0:48], T.kf[:, h:h + 1], T.fb[:, 2 + h:3 + h], A.is_equal, A.mult))
+        V(ts(T.bb[:, 96 * h + 48:96 * h + 96], T.rowj[:, 0:48], T.kf[:, h:h + 1], T.fb[:, 4 + h:5 + h], A.is_equal, A.mult))
+    g.tensor.wait_ge(S.v, level())
     g.tensor.matmul(T.ps2[:, 0:48], T.a0[:, :], T.bb[:, 0:48], True, False)
-    V(vec.tensor_scalar(T.a1[:, :], T.i16[:, :], T.kf[:, 3:4], T.fb[:, 3:4], A.is_equal, A.mult))
-    h1 = V(vec.tensor_scalar(T.bb[:, 48:96], T.rowj[:, 0:48], T.kf[:, 1:2], None, A.is_equal))
-    g.tensor.wait_ge(S.v, h1)
-    g.tensor.matmul(T.ps2[:, 0:48], T.a1[:, :], T.bb[:, 48:96], False, True).then_inc(S.p, 1)
+    g.tensor.matmul(T.ps2[:, 0:48], T.a0[:, :], T.bb[:, 48:96], False, False)
+    g.tensor.matmul(T.ps2[:, 0:48], T.a1[:, :], T.bb[:, 96:144], False, False)
+    g.tensor.matmul(T.ps2[:, 0:48], T.a1[:, :], T.bb[:, 144:192], False, True).then_inc(S.p, 1)
     vec.wait_ge(S.p, 3)
-    req_done = V(vec.tensor_copy(T.req[:, :], T.ps2[:, 0:48]))
+    V(vec.tensor_copy(T.req[:, :], T.ps2[:, 0:48]))
 
-    g.wait_ge(S.v, req_done)
+    g.wait_ge(S.v, level())
     _emit(g, T, topo, core, snd["qfeed"])
     _emit(g, T, topo, core, snd["qdir"])
 
-    V(vec.tensor_tensor(T.posf[:, :], T.kk[:, :], T.o64[:, :], A.add))
-    V(vec.tensor_scalar(T.pb[:, 0:1], T.pci[:, :], 3, None, A.arith_shift_right))
-    V(vec.tensor_scalar(T.pb[:, 1:2], T.pci[:, :], 7, None, A.bitwise_and))
+    V(ts(T.pb[:, 0:1], T.pci[:, :], 3, None, A.arith_shift_right))
+    V(ts(T.pb[:, 1:2], T.pci[:, :], 7, None, A.bitwise_and))
+    level()
     V(vec.tensor_copy(T.pbf[:, :], T.pb[:, :]))
-    V(vec.tensor_scalar(T.pm[:, :], T.i16[:, :], T.pbf[:, 0:1], None, A.is_equal))
+    level()
+    V(ts(T.pm[:, :], T.i16[:, :], T.pbf[:, 0:1], None, A.is_equal))
     for h in range(2):
-        V(vec.tensor_scalar(T.cc[:, h:h + 1], T.pbf[:, 1:2], 2.0, float(h), A.mult, A.add))
+        V(ts(T.cc[:, h:h + 1], T.pbf[:, 1:2], 2.0, float(h), A.mult, A.add))
+    level()
     for h in range(2):
-        V(vec.tensor_scalar(T.cm[:, 16 * h:16 * h + 16], T.rowj[:, 0:16], T.cc[:, h:h + 1], None, A.is_equal))
-    V(vec.tensor_scalar(T.a2[:, :], T.pm[:, :], T.posf[:, 0:1], None, A.mult))
-    f1 = V(vec.tensor_scalar(T.a3[:, :], T.pm[:, :], T.posf[:, 1:2], None, A.mult))
-    g.tensor.wait_ge(S.v, f1)
+        V(ts(T.cm[:, 16 * h:16 * h + 16], T.rowj[:, 0:16], T.cc[:, h:h + 1], None, A.is_equal))
+    V(ts(T.a2[:, :], T.pm[:, :], T.posf[:, 0:1], None, A.mult))
+    V(ts(T.a3[:, :], T.pm[:, :], T.posf[:, 1:2], None, A.mult))
+    g.tensor.wait_ge(S.v, level())
     g.tensor.matmul(T.ps3[:, 0:16], T.a2[:, :], T.cm[:, 0:16], True, False)
     g.tensor.matmul(T.ps3[:, 0:16], T.a3[:, :], T.cm[:, 16:32], False, True).then_inc(S.p, 1)
     vec.wait_ge(S.p, 4)
     V(vec.tensor_copy(T.fo[:, :], T.ps3[:, 0:16]))
 
+    nh = nx // 2
     g.scalar.wait_ge(S.stab, 16)
     g.scalar.wait_ge(S.rqs, P["expect"][(core, "rqs")])
-    g.scalar.activation(T.gs[:, 0:CAP * ns], T.tabs[:, :].indirect(T.offs[:, 0:4 * ns]),
-                        ActivationFunctionType.Copy).then_inc(S.a, 1)
+    g.scalar.activation(T.gs[:, 0:CAP * ns], T.tabs[:, :].indirect(T.offs[:, 0:4 * ns]), Copy).then_inc(S.a, 1)
+    g.scalar.wait_ge(S.a, 1)
+    g.scalar.wait_ge(S.rqx, P["expect"][(core, "rqx")])
+    g.scalar.activation(T.gx[:, CAP * nh:CAP * nx], T.tabs[:, :].indirect(T.offx[:, 4 * nh:4 * nx]), Copy).then_inc(S.a, 1)
     vec.wait_ge(S.stab, 16)
     V(vec.tensor_copy(T.land[:, CAP * rank:CAP * rank + CAP], T.tabs[:, :].indirect(T.req[:, 4 * rank:4 * rank + 4])))
     vec.wait_ge(S.rqx, P["expect"][(core, "rqx")])
-    gx_done = V(vec.tensor_copy(T.gx[:, 0:CAP * nx], T.tabs[:, :].indirect(T.offx[:, 0:4 * nx])))
+    V(vec.tensor_copy(T.gx[:, 0:CAP * nh], T.tabs[:, :].indirect(T.offx[:, 0:4 * nh])))
+    gx_done = level()
 
     g.wait_ge(S.a, 1)
     _emit(g, T, topo, core, snd["rdir"])
     g.wait_ge(S.v, gx_done)
+    g.wait_ge(S.a, 2)
     _emit(g, T, topo, core, snd["rfeed"])
 
     vec.wait_ge(S.sx, 16)
     vec.wait_ge(S.lnd, P["expect"][(core, "lnd")])
-    y_done = V(vec.tensor_tensor(T.ys[:, :], T.land[:, :].indirect(T.fo[:, :]), T.xs[:, :], A.add))
-    g.sync.wait_ge(S.v, y_done)
+    V(vec.tensor_tensor(T.ys[:, :], T.land[:, :].indirect(T.fo[:, :]), T.xs[:, :], A.add))
+    g.sync.wait_ge(S.v, level())
     g.sync.dma_start(T.y[:, :], T.ys[:, :]).then_inc(S.sy, 16)
     g.sync.wait_ge(S.sy, 16)
     g.wait_ge(S.ls, P["local"][core])

@@ -53,7 +53,8 @@ SCRATCH = {
     "ps2": ("psum", [128, 512], "float32"),
     "ps3": ("psum", [128, 512], "float32"),
 }
-SEMAPHORES = ["sidx", "stab", "sx", "sy", "gi", "v", "p", "a", "ls", "fq", "fr", "rqs", "rqx", "lnd"]
+SEMAPHORES = ["sidx", "stab", "sx", "sy", "ga", "gb", "gk", "v", "p", "ls", "fq", "fr", "rqs", "rqx", "lnd",
+              "e0", "h0", "c0", "c1", "c2", "cx", "slf"]
 
 _memo = {}
 
@@ -166,30 +167,38 @@ def rank_program(g, core, T, topo):
     g.sync.dma_start(T.tabs[:, :], T.tab[:, :]).then_inc(S.stab, 16)
     g.sync.dma_start(T.xs[:, :], T.x[:, :]).then_inc(S.sx, 16)
 
-    g.iota(T.rowj[:, :], [[1, 128]], 0, 0, allow_small_or_imprecise_dtypes=True).then_inc(S.gi, 1)
-    g.iota(T.pci[:, :], [[0, 1]], 0, 1).then_inc(S.gi, 1)
-    g.iota(T.i16[:, :], [[0, 8], [1, 16]], 0, 0, allow_small_or_imprecise_dtypes=True).then_inc(S.gi, 1)
+    g.iota(T.pci[:, :], [[0, 1]], 0, 1).then_inc(S.ga, 1)
+    g.iota(T.rowj[:, :], [[1, 128]], 0, 0, allow_small_or_imprecise_dtypes=True).then_inc(S.gb, 1)
+    g.iota(T.i16[:, :], [[0, 8], [1, 16]], 0, 0, allow_small_or_imprecise_dtypes=True).then_inc(S.gk, 1)
     V(vec.memset(T.ones[:, :], 1.0))
-    vec.wait_ge(S.gi, 3)
+    vec.wait_ge(S.ga, 1)
     V(vec.tensor_copy(T.pcf[:, :], T.pci[:, :]))
+    V(ts(T.pb[:, 0:1], T.pci[:, :], 3, None, A.arith_shift_right))
+    V(ts(T.pb[:, 1:2], T.pci[:, :], 7, None, A.bitwise_and))
     level()
+    vec.wait_ge(S.gb, 1)
     V(ts(T.ltri[:, :], T.rowj[:, :], T.pcf[:, 0:1], None, A.is_gt))
-    level()
+    V(vec.tensor_copy(T.pbf[:, :], T.pb[:, :]))
 
     vec.wait_ge(S.sidx, 16)
     V(ts(T.ib[:, 0:2], T.idxs[:, :], 12, None, A.arith_shift_right))
-    V(ts(T.ib[:, 2:4], T.idxs[:, :], RP - CAP, None, A.bitwise_and))
-    V(ts(T.ib[:, 4:6], T.idxs[:, :], CAP - 1, None, A.bitwise_and))
     level()
-    V(vec.tensor_copy(T.fb[:, :], T.ib[:, :]))
-    level()
-    V(ts(T.eh[:, 0:16], T.rowj[:, 0:16], T.fb[:, 0:1], None, A.is_equal))
+    V(vec.tensor_copy(T.fb[:, 0:2], T.ib[:, 0:2]))
+    consts = level()
+    ts(T.eh[:, 0:16], T.rowj[:, 0:16], T.fb[:, 0:1], None, A.is_equal).then_inc(S.e0, 1)
     V(ts(T.eh[:, 16:32], T.rowj[:, 0:16], T.fb[:, 1:2], None, A.is_equal))
-    V(ts(T.o64[:, :], T.fb[:, 0:2], float(CAP), None, A.mult))
-    g.tensor.wait_ge(S.v, level())
+    g.tensor.wait_ge(S.v, consts)
+    g.tensor.wait_ge(S.e0, 1)
     g.tensor.matmul(T.ps1[:, 0:16], T.ltri[:, :], T.eh[:, 0:16], True, True).then_inc(S.p, 1)
     g.tensor.matmul(T.ps1[:, 16:32], T.ones[:, :], T.eh[:, 0:16], True, False)
+    g.tensor.wait_ge(S.v, level())
     g.tensor.matmul(T.ps1[:, 16:32], T.ltri[:, :], T.eh[:, 16:32], False, True).then_inc(S.p, 1)
+    vec.wait_ge(S.e0, 1)
+    V(ts(T.ib[:, 2:4], T.idxs[:, :], RP - CAP, None, A.bitwise_and))
+    V(ts(T.ib[:, 4:6], T.idxs[:, :], CAP - 1, None, A.bitwise_and))
+    V(ts(T.o64[:, :], T.fb[:, 0:2], float(CAP), None, A.mult))
+    level()
+    V(vec.tensor_copy(T.fb[:, 2:6], T.ib[:, 2:6]))
     vec.wait_ge(S.p, 2)
     V(vec.tensor_tensor(T.ec[:, :], T.eh[:, :], T.ps1[:, 0:32], A.mult))
     level()
@@ -197,34 +206,37 @@ def rank_program(g, core, T, topo):
     V(vec.tensor_reduce(T.kk[:, 1:2], T.ec[:, 16:32], AxisListType.X, A.add))
     level()
     V(vec.tensor_tensor(T.posi[:, :], T.kk[:, :], T.o64[:, :], A.add))
-    V(vec.tensor_tensor(T.posf[:, :], T.kk[:, :], T.o64[:, :], A.add))
     level()
     V(ts(T.kb[:, 0:2], T.posi[:, :], 4, None, A.arith_shift_right))
     V(ts(T.kb[:, 2:4], T.posi[:, :], 15, None, A.bitwise_and))
     level()
     V(vec.tensor_copy(T.kf[:, :], T.kb[:, :]))
     level()
+    vec.wait_ge(S.gk, 1)
     for h, ah in enumerate((T.a0, T.a1)):
-        V(ts(ah[:, :], T.i16[:, :], T.kf[:, 2 + h:3 + h], None, A.is_equal))
-        V(ts(T.bb[:, 96 * h:96 * h + 48], T.rowj[:, 0:48], T.kf[:, h:h + 1], T.fb[:, 2 + h:3 + h], A.is_equal, A.mult))
-        V(ts(T.bb[:, 96 * h + 48:96 * h + 96], T.rowj[:, 0:48], T.kf[:, h:h + 1], T.fb[:, 4 + h:5 + h], A.is_equal, A.mult))
-    g.tensor.wait_ge(S.v, level())
+        ins = [ts(ah[:, :], T.i16[:, :], T.kf[:, 2 + h:3 + h], None, A.is_equal),
+               ts(T.bb[:, 96 * h:96 * h + 48], T.rowj[:, 0:48], T.kf[:, h:h + 1], T.fb[:, 2 + h:3 + h], A.is_equal, A.mult),
+               ts(T.bb[:, 96 * h + 48:96 * h + 96], T.rowj[:, 0:48], T.kf[:, h:h + 1], T.fb[:, 4 + h:5 + h], A.is_equal, A.mult)]
+        for i in ins:
+            if h == 0:
+                i.then_inc(S.h0, 1)
+            else:
+                V(i)
+    g.tensor.wait_ge(S.h0, 3)
     g.tensor.matmul(T.ps2[:, 0:48], T.a0[:, :], T.bb[:, 0:48], True, False)
     g.tensor.matmul(T.ps2[:, 0:48], T.a0[:, :], T.bb[:, 48:96], False, False)
+    g.tensor.wait_ge(S.v, level())
     g.tensor.matmul(T.ps2[:, 0:48], T.a1[:, :], T.bb[:, 96:144], False, False)
     g.tensor.matmul(T.ps2[:, 0:48], T.a1[:, :], T.bb[:, 144:192], False, True).then_inc(S.p, 1)
+    V(vec.tensor_tensor(T.posf[:, :], T.kk[:, :], T.o64[:, :], A.add))
     vec.wait_ge(S.p, 3)
     V(vec.tensor_copy(T.req[:, :], T.ps2[:, 0:48]))
 
-    g.wait_ge(S.v, level())
+    req_done = level()
+    g.wait_ge(S.v, req_done)
     _emit(g, T, topo, core, snd["qfeed"])
     _emit(g, T, topo, core, snd["qdir"])
 
-    V(ts(T.pb[:, 0:1], T.pci[:, :], 3, None, A.arith_shift_right))
-    V(ts(T.pb[:, 1:2], T.pci[:, :], 7, None, A.bitwise_and))
-    level()
-    V(vec.tensor_copy(T.pbf[:, :], T.pb[:, :]))
-    level()
     V(ts(T.pm[:, :], T.i16[:, :], T.pbf[:, 0:1], None, A.is_equal))
     for h in range(2):
         V(ts(T.cc[:, h:h + 1], T.pbf[:, 1:2], 2.0, float(h), A.mult, A.add))
@@ -239,26 +251,37 @@ def rank_program(g, core, T, topo):
     vec.wait_ge(S.p, 4)
     V(vec.tensor_copy(T.fo[:, :], T.ps3[:, 0:16]))
 
-    nh = nx // 2
+    g.scalar.wait_ge(S.v, req_done)
     g.scalar.wait_ge(S.stab, 16)
-    g.scalar.wait_ge(S.rqs, P["expect"][(core, "rqs")])
-    g.scalar.activation(T.gs[:, 0:CAP * ns], T.tabs[:, :].indirect(T.offs[:, 0:4 * ns]), Copy).then_inc(S.a, 1)
-    g.scalar.wait_ge(S.a, 1)
-    g.scalar.wait_ge(S.rqx, P["expect"][(core, "rqx")])
-    g.scalar.activation(T.gx[:, CAP * nh:CAP * nx], T.tabs[:, :].indirect(T.offx[:, 4 * nh:4 * nx]), Copy).then_inc(S.a, 1)
+    g.scalar.activation(T.land[:, CAP * rank:CAP * rank + CAP], T.tabs[:, :].indirect(T.req[:, 4 * rank:4 * rank + 4]), Copy).then_inc(S.slf, 1)
     vec.wait_ge(S.stab, 16)
-    V(vec.tensor_copy(T.land[:, CAP * rank:CAP * rank + CAP], T.tabs[:, :].indirect(T.req[:, 4 * rank:4 * rank + 4])))
+    vec.wait_ge(S.rqs, P["expect"][(core, "rqs")])
+    g.scalar.wait_ge(S.rqs, P["expect"][(core, "rqs")])
+    parts, b0 = [], 0
+    for ci, call in enumerate(snd["rdir"]):
+        b1 = b0 + len(call)
+        bm = (b0 + b1 + 1) // 2
+        sem = S["c%d" % ci]
+        vec.tensor_copy(T.gs[:, CAP * b0:CAP * bm], T.tabs[:, :].indirect(T.offs[:, 4 * b0:4 * bm])).then_inc(sem, 1)
+        if b1 > bm:
+            g.scalar.activation(T.gs[:, CAP * bm:CAP * b1], T.tabs[:, :].indirect(T.offs[:, 4 * bm:4 * b1]), Copy).then_inc(sem, 1)
+        parts.append((sem, 2 if b1 > bm else 1))
+        b0 = b1
+    nh = nx // 2
     vec.wait_ge(S.rqx, P["expect"][(core, "rqx")])
-    V(vec.tensor_copy(T.gx[:, 0:CAP * nh], T.tabs[:, :].indirect(T.offx[:, 0:4 * nh])))
-    gx_done = level()
+    g.scalar.wait_ge(S.rqx, P["expect"][(core, "rqx")])
+    vec.tensor_copy(T.gx[:, 0:CAP * nh], T.tabs[:, :].indirect(T.offx[:, 0:4 * nh])).then_inc(S.cx, 1)
+    g.scalar.activation(T.gx[:, CAP * nh:CAP * nx], T.tabs[:, :].indirect(T.offx[:, 4 * nh:4 * nx]), Copy).then_inc(S.cx, 1)
 
-    g.wait_ge(S.a, 1)
-    _emit(g, T, topo, core, snd["rdir"])
-    g.wait_ge(S.v, gx_done)
-    g.wait_ge(S.a, 2)
+    for ci, (sem, cnt) in enumerate(parts):
+        g.wait_ge(sem, cnt)
+        _emit(g, T, topo, core, [snd["rdir"][ci]])
+    g.wait_ge(S.cx, 2)
     _emit(g, T, topo, core, snd["rfeed"])
 
+    level()
     vec.wait_ge(S.sx, 16)
+    vec.wait_ge(S.slf, 1)
     vec.wait_ge(S.lnd, P["expect"][(core, "lnd")])
     V(vec.tensor_tensor(T.ys[:, :], T.land[:, :].indirect(T.fo[:, :]), T.xs[:, :], A.add))
     g.sync.wait_ge(S.v, level())

@@ -8,6 +8,8 @@ TT = 256
 CAP = 64
 NSIM = 256
 GRP = 2
+NCH = 4
+POR = 4
 
 SCRATCH = {
     "idxs": ("sbuf", [128, 2], "int32"),
@@ -48,13 +50,13 @@ SCRATCH = {
     "gx": ("sbuf", [128, CAP * N], "bfloat16"),
     "land": ("sbuf", [128, CAP * N], "bfloat16"),
     "rq": ("sbuf", [128, 4 * N], "uint16"),
-    "rl": ("sbuf", [128, CAP * GRP], "bfloat16"),
     "ps1": ("psum", [128, 512], "float32"),
     "ps2": ("psum", [128, 512], "float32"),
     "ps3": ("psum", [128, 512], "float32"),
 }
-SEMAPHORES = ["sidx", "stab", "sx", "sy", "ga", "gb", "gk", "v", "p", "ls", "fq", "fr", "rqs", "rqx", "lnd",
-              "e0", "h0", "c0", "c1", "c2", "cx", "slf"]
+SEMAPHORES = ["sidx", "stab0", "stab1", "stab2", "stab3", "sx", "sy", "ga", "gb", "gk", "v", "p", "ls", "fq",
+              "tb0", "tb1", "tb2", "tb3", "rqs", "rqx", "lnd",
+              "e0", "h0", "c0", "c1", "c2", "slf"]
 
 _memo = {}
 
@@ -63,11 +65,11 @@ def _engines(mask):
     return [e for e in range(16) if (mask >> e) & 1]
 
 
-def _calls(items, engs):
+def _calls(items, engs, most=16):
     out, i = [], 0
     while i < len(items):
         t = 1
-        while t * 2 <= min(len(items) - i, len(engs)):
+        while t * 2 <= min(len(items) - i, len(engs), most):
             t *= 2
         w = len(engs) // t
         out.append([(sum(1 << e for e in engs[j * w:(j + 1) * w]),) + tuple(items[i + j]) for j in range(t)])
@@ -79,7 +81,7 @@ def plan(cores, topo):
     if "p" in _memo:
         return _memo["p"]
     n = len(cores)
-    same, cross, relays, groups = [], [], [], []
+    same, cross, relays, groups, servers = [], [], [], [], []
     for r, c in enumerate(cores):
         ring = [(r + 1 + i) % n for i in range(n - 1)]
         same.append([s for s in ring if topo.same_plane(c, cores[s])])
@@ -90,10 +92,11 @@ def plan(cores, topo):
         k = min(len(cand), (len(cross[r]) + GRP - 1) // GRP)
         relays.append(cand[:k])
         groups.append([cross[r][i * GRP:(i + 1) * GRP] for i in range(k)])
+        servers.append(cand[:(len(cross[r]) + POR - 1) // POR])
     sends, expect, local, role = {}, {}, {}, {}
 
-    def add(core, phase, items, engs):
-        cs = _calls(items, engs)
+    def add(core, phase, items, engs, most=16):
+        cs = _calls(items, engs, most)
         sends.setdefault(core, {})[phase] = cs
         for call in cs:
             for (mask, d, sem, s, t) in call:
@@ -101,24 +104,32 @@ def plan(cores, topo):
                 expect[(d, sem)] = expect.get((d, sem), 0) + e
                 local[core] = local.get(core, 0) + e
 
+    def desk(s, r):
+        i = cross[s].index(r)
+        return servers[s][i // POR], i % POR
+
     for r, c in enumerate(cores):
         off = _engines(topo.mask(c, cores[same[r][0]]))
         onc = _engines(topo.mask(c, relays[r][0]))
-        rest = [e for e in onc if e not in off]
+        line = [c] + servers[r]
+        for i in range(NCH):
+            a, b = RP * i // NCH, RP * (i + 1) // NCH
+            for u, w in zip(line[:-1], line[1:]):
+                add(u, "tab%d" % i, [(w, "tb%d" % i, ("tabs", a, b), ("tabs", a, b))], _engines(topo.mask(u, w)))
         add(c, "qfeed", [(d, "fq", ("req", 0, 4 * n), ("rq", 0, 4 * n)) for d in relays[r]], onc)
         add(c, "qdir", [(cores[s], "rqs", ("req", 4 * s, 4 * s + 4), ("offs", 4 * same[s].index(r), 4 * same[s].index(r) + 4))
                         for s in same[r]], off)
         add(c, "rdir", [(cores[s], "lnd", ("gs", CAP * i, CAP * i + CAP), ("land", CAP * r, CAP * r + CAP))
                         for i, s in enumerate(same[r])], off)
-        add(c, "rfeed", [(d, "fr", ("gx", CAP * GRP * i, CAP * GRP * (i + 1)), ("rl", 0, CAP * GRP))
-                         for i, d in enumerate(relays[r])], onc if len(same[r]) < len(cross[r]) else rest)
         for i, d in enumerate(relays[r]):
             role[d] = r
-            eo = _engines(topo.mask(d, cores[groups[r][i][0]]))
-            add(d, "q", [(cores[s], "rqx", ("rq", 4 * s, 4 * s + 4), ("offx", 4 * cross[s].index(r), 4 * cross[s].index(r) + 4))
+            eo = _engines(topo.mask(d, desk(groups[r][i][0], r)[0]))
+            add(d, "q", [(desk(s, r)[0], "rqx", ("rq", 4 * s, 4 * s + 4), ("offx", 4 * desk(s, r)[1], 4 * desk(s, r)[1] + 4))
                          for s in groups[r][i]], eo)
-            add(d, "r", [(cores[s], "lnd", ("rl", CAP * j, CAP * j + CAP), ("land", CAP * r, CAP * r + CAP))
-                         for j, s in enumerate(groups[r][i])], eo)
+        for j, d in enumerate(servers[r]):
+            mine = cross[r][POR * j:POR * (j + 1)]
+            add(d, "r", [(cores[s], "lnd", ("gx", CAP * i, CAP * i + CAP), ("land", CAP * r, CAP * r + CAP))
+                         for i, s in enumerate(mine)], _engines(topo.mask(d, cores[mine[0]])), POR)
     _memo["p"] = dict(same=same, cross=cross, sends=sends, expect=expect, local=local, role=role)
     return _memo["p"]
 
@@ -133,6 +144,24 @@ def _emit(g, T, topo, core, calls):
         g.remote_dma_fused(trs, local_sem=T.sem.ls)
 
 
+def _serve(g, T, topo, core, calls, out, offs):
+    S = T.sem
+    Copy = ActivationFunctionType.Copy
+    parts, b0 = [], 0
+    for ci, call in enumerate(calls):
+        b1 = b0 + len(call)
+        bm = (b0 + b1 + 1) // 2
+        sem = S["c%d" % ci]
+        g.vector.tensor_copy(out[:, CAP * b0:CAP * bm], T.tabs[:, :].indirect(offs[:, 4 * b0:4 * bm])).then_inc(sem, 1)
+        if b1 > bm:
+            g.scalar.activation(out[:, CAP * bm:CAP * b1], T.tabs[:, :].indirect(offs[:, 4 * bm:4 * b1]), Copy).then_inc(sem, 1)
+        parts.append((sem, 2 if b1 > bm else 1))
+        b0 = b1
+    for ci, (sem, cnt) in enumerate(parts):
+        g.wait_ge(sem, cnt)
+        _emit(g, T, topo, core, [calls[ci]])
+
+
 def rank_program(g, core, T, topo):
     P = plan(list(T.cores), topo)
     rank = T.rank_of(core)
@@ -140,16 +169,24 @@ def rank_program(g, core, T, topo):
     if rank is None:
         if core not in P["role"]:
             return
+        snd = P["sends"][core]
+        for i in range(NCH):
+            if "tab%d" % i in snd:
+                g.wait_ge(S["tb%d" % i], P["expect"][(core, "tb%d" % i)])
+                _emit(g, T, topo, core, snd["tab%d" % i])
         g.wait_ge(S.fq, P["expect"][(core, "fq")])
-        _emit(g, T, topo, core, P["sends"][core]["q"])
-        g.wait_ge(S.fr, P["expect"][(core, "fr")])
-        _emit(g, T, topo, core, P["sends"][core]["r"])
+        _emit(g, T, topo, core, snd["q"])
+        if "r" in snd:
+            for q in (g.vector, g.scalar):
+                for i in range(NCH):
+                    q.wait_ge(S["tb%d" % i], P["expect"][(core, "tb%d" % i)])
+                q.wait_ge(S.rqx, P["expect"][(core, "rqx")])
+            _serve(g, T, topo, core, snd["r"], T.gx, T.offx)
         g.wait_ge(S.ls, P["local"][core])
         return
 
     A = AluOpType
     Copy = ActivationFunctionType.Copy
-    ns, nx = len(P["same"][rank]), len(P["cross"][rank])
     snd = P["sends"][core]
     nv = [0]
     vec = g.vector
@@ -164,12 +201,18 @@ def rank_program(g, core, T, topo):
         return nv[0]
 
     g.sync.dma_start(T.idxs[:, :], T.idx[:, :]).then_inc(S.sidx, 16)
-    g.sync.dma_start(T.tabs[:, :], T.tab[:, :]).then_inc(S.stab, 16)
+    for i in range(NCH):
+        a, b = RP * i // NCH, RP * (i + 1) // NCH
+        g.sync.dma_start(T.tabs[:, a:b], T.tab[:, a:b]).then_inc(S["stab%d" % i], 16)
     g.sync.dma_start(T.xs[:, :], T.x[:, :]).then_inc(S.sx, 16)
 
     g.iota(T.pci[:, :], [[0, 1]], 0, 1).then_inc(S.ga, 1)
     g.iota(T.rowj[:, :], [[1, 128]], 0, 0, allow_small_or_imprecise_dtypes=True).then_inc(S.gb, 1)
     g.iota(T.i16[:, :], [[0, 8], [1, 16]], 0, 0, allow_small_or_imprecise_dtypes=True).then_inc(S.gk, 1)
+    for i in range(NCH):
+        g.wait_ge(S["stab%d" % i], 16)
+        _emit(g, T, topo, core, snd["tab%d" % i])
+
     V(vec.memset(T.ones[:, :], 1.0))
     vec.wait_ge(S.ga, 1)
     V(vec.tensor_copy(T.pcf[:, :], T.pci[:, :]))
@@ -252,32 +295,13 @@ def rank_program(g, core, T, topo):
     V(vec.tensor_copy(T.fo[:, :], T.ps3[:, 0:16]))
 
     g.scalar.wait_ge(S.v, req_done)
-    g.scalar.wait_ge(S.stab, 16)
+    for i in range(NCH):
+        g.scalar.wait_ge(S["stab%d" % i], 16)
+        vec.wait_ge(S["stab%d" % i], 16)
     g.scalar.activation(T.land[:, CAP * rank:CAP * rank + CAP], T.tabs[:, :].indirect(T.req[:, 4 * rank:4 * rank + 4]), Copy).then_inc(S.slf, 1)
-    vec.wait_ge(S.stab, 16)
     vec.wait_ge(S.rqs, P["expect"][(core, "rqs")])
     g.scalar.wait_ge(S.rqs, P["expect"][(core, "rqs")])
-    parts, b0 = [], 0
-    for ci, call in enumerate(snd["rdir"]):
-        b1 = b0 + len(call)
-        bm = (b0 + b1 + 1) // 2
-        sem = S["c%d" % ci]
-        vec.tensor_copy(T.gs[:, CAP * b0:CAP * bm], T.tabs[:, :].indirect(T.offs[:, 4 * b0:4 * bm])).then_inc(sem, 1)
-        if b1 > bm:
-            g.scalar.activation(T.gs[:, CAP * bm:CAP * b1], T.tabs[:, :].indirect(T.offs[:, 4 * bm:4 * b1]), Copy).then_inc(sem, 1)
-        parts.append((sem, 2 if b1 > bm else 1))
-        b0 = b1
-    nh = nx // 2
-    vec.wait_ge(S.rqx, P["expect"][(core, "rqx")])
-    g.scalar.wait_ge(S.rqx, P["expect"][(core, "rqx")])
-    vec.tensor_copy(T.gx[:, 0:CAP * nh], T.tabs[:, :].indirect(T.offx[:, 0:4 * nh])).then_inc(S.cx, 1)
-    g.scalar.activation(T.gx[:, CAP * nh:CAP * nx], T.tabs[:, :].indirect(T.offx[:, 4 * nh:4 * nx]), Copy).then_inc(S.cx, 1)
-
-    for ci, (sem, cnt) in enumerate(parts):
-        g.wait_ge(sem, cnt)
-        _emit(g, T, topo, core, [snd["rdir"][ci]])
-    g.wait_ge(S.cx, 2)
-    _emit(g, T, topo, core, snd["rfeed"])
+    _serve(g, T, topo, core, snd["rdir"], T.gs, T.offs)
 
     level()
     vec.wait_ge(S.sx, 16)

@@ -7,9 +7,9 @@ RP = 4096
 TT = 256
 CAP = 64
 NSIM = 256
-GRP = 2
+NSV = 2
 NCH = 4
-POR = 4
+MOST = 4
 
 SCRATCH = {
     "idxs": ("sbuf", [128, 2], "int32"),
@@ -56,7 +56,7 @@ SCRATCH = {
 }
 SEMAPHORES = ["sidx", "stab0", "stab1", "stab2", "stab3", "sx", "sy", "ga", "gb", "gk", "v", "p", "ls", "fq",
               "tb0", "tb1", "tb2", "tb3", "rqs", "rqx", "lnd",
-              "e0", "h0", "c0", "c1", "c2", "slf"]
+              "e0", "h0", "c0", "c1", "c2", "c3", "slf"]
 
 _memo = {}
 
@@ -65,11 +65,11 @@ def _engines(mask):
     return [e for e in range(16) if (mask >> e) & 1]
 
 
-def _calls(items, engs, most=16):
+def _calls(items, engs):
     out, i = [], 0
     while i < len(items):
         t = 1
-        while t * 2 <= min(len(items) - i, len(engs), most):
+        while t * 2 <= min(len(items) - i, len(engs)):
             t *= 2
         w = len(engs) // t
         out.append([(sum(1 << e for e in engs[j * w:(j + 1) * w]),) + tuple(items[i + j]) for j in range(t)])
@@ -81,7 +81,7 @@ def plan(cores, topo):
     if "p" in _memo:
         return _memo["p"]
     n = len(cores)
-    same, cross, relays, groups, servers = [], [], [], [], []
+    same, cross, servers, per, kept, lent = [], [], [], [], [], []
     for r, c in enumerate(cores):
         ring = [(r + 1 + i) % n for i in range(n - 1)]
         same.append([s for s in ring if topo.same_plane(c, cores[s])])
@@ -89,14 +89,18 @@ def plan(cores, topo):
         cand = [d for d in range(NSIM) if d not in cores and topo.host(d) == topo.host(c) and topo.chip(d) == topo.chip(c)
                 and all(topo.may_write(d, cores[s]) for s in cross[r])]
         cand.sort(key=lambda d: (topo.die(d) != topo.die(c), d))
-        k = min(len(cand), (len(cross[r]) + GRP - 1) // GRP)
-        relays.append(cand[:k])
-        groups.append([cross[r][i * GRP:(i + 1) * GRP] for i in range(k)])
-        servers.append(cand[:(len(cross[r]) + POR - 1) // POR])
+        servers.append(cand[:NSV])
+        per.append((len(cross[r]) + NSV - 1) // NSV)
+        room = max(0, MOST - per[r])
+        k = max(len(same[r]) - NSV * room, 0)
+        kept.append(same[r][:k])
+        lent.append([same[r][k + room * j:k + room * (j + 1)] for j in range(NSV)])
     sends, expect, local, role = {}, {}, {}, {}
 
-    def add(core, phase, items, engs, most=16):
-        cs = _calls(items, engs, most)
+    def add(core, phase, items, engs):
+        if not items:
+            return
+        cs = _calls(items, engs)
         sends.setdefault(core, {})[phase] = cs
         for call in cs:
             for (mask, d, sem, s, t) in call:
@@ -106,31 +110,40 @@ def plan(cores, topo):
 
     def desk(s, r):
         i = cross[s].index(r)
-        return servers[s][i // POR], i % POR
+        return servers[s][i // per[s]], i % per[s]
+
+    def counter(s, r):
+        if r in kept[s]:
+            return cores[s], kept[s].index(r)
+        for j in range(NSV):
+            if r in lent[s][j]:
+                return servers[s][j], lent[s][j].index(r)
 
     for r, c in enumerate(cores):
         off = _engines(topo.mask(c, cores[same[r][0]]))
-        onc = _engines(topo.mask(c, relays[r][0]))
-        line = [c] + servers[r]
+        onc = _engines(topo.mask(c, servers[r][0]))
         for i in range(NCH):
             a, b = RP * i // NCH, RP * (i + 1) // NCH
-            for u, w in zip(line[:-1], line[1:]):
-                add(u, "tab%d" % i, [(w, "tb%d" % i, ("tabs", a, b), ("tabs", a, b))], _engines(topo.mask(u, w)))
-        add(c, "qfeed", [(d, "fq", ("req", 0, 4 * n), ("rq", 0, 4 * n)) for d in relays[r]], onc)
-        add(c, "qdir", [(cores[s], "rqs", ("req", 4 * s, 4 * s + 4), ("offs", 4 * same[s].index(r), 4 * same[s].index(r) + 4))
+            u = servers[r][i % NSV]
+            add(c, "tab%d" % i, [(u, "tb%d" % i, ("tabs", a, b), ("tabs", a, b))], onc)
+            add(u, "tab%d" % i, [(w, "tb%d" % i, ("tabs", a, b), ("tabs", a, b)) for w in servers[r] if w != u],
+                _engines(topo.mask(u, servers[r][(i + 1) % NSV])))
+        add(c, "qfeed", [(d, "fq", ("req", 0, 4 * n), ("rq", 0, 4 * n)) for d in servers[r]], onc)
+        add(c, "qdir", [(counter(s, r)[0], "rqs", ("req", 4 * s, 4 * s + 4), ("offs", 4 * counter(s, r)[1], 4 * counter(s, r)[1] + 4))
                         for s in same[r]], off)
         add(c, "rdir", [(cores[s], "lnd", ("gs", CAP * i, CAP * i + CAP), ("land", CAP * r, CAP * r + CAP))
-                        for i, s in enumerate(same[r])], off)
-        for i, d in enumerate(relays[r]):
-            role[d] = r
-            eo = _engines(topo.mask(d, desk(groups[r][i][0], r)[0]))
-            add(d, "q", [(desk(s, r)[0], "rqx", ("rq", 4 * s, 4 * s + 4), ("offx", 4 * desk(s, r)[1], 4 * desk(s, r)[1] + 4))
-                         for s in groups[r][i]], eo)
+                        for i, s in enumerate(kept[r])], off)
         for j, d in enumerate(servers[r]):
-            mine = cross[r][POR * j:POR * (j + 1)]
+            role[d] = r
+            mine = cross[r][per[r] * j:per[r] * (j + 1)]
+            eo = _engines(topo.mask(d, cores[mine[0]]))
+            add(d, "q", [(desk(s, r)[0], "rqx", ("rq", 4 * s, 4 * s + 4), ("offx", 4 * desk(s, r)[1], 4 * desk(s, r)[1] + 4))
+                         for s in mine], eo)
+            add(d, "rs", [(cores[s], "lnd", ("gs", CAP * i, CAP * i + CAP), ("land", CAP * r, CAP * r + CAP))
+                          for i, s in enumerate(lent[r][j])], eo)
             add(d, "r", [(cores[s], "lnd", ("gx", CAP * i, CAP * i + CAP), ("land", CAP * r, CAP * r + CAP))
-                         for i, s in enumerate(mine)], _engines(topo.mask(d, cores[mine[0]])), POR)
-    _memo["p"] = dict(same=same, cross=cross, sends=sends, expect=expect, local=local, role=role)
+                         for i, s in enumerate(mine)], eo)
+    _memo["p"] = dict(sends=sends, expect=expect, local=local, role=role)
     return _memo["p"]
 
 
@@ -144,14 +157,14 @@ def _emit(g, T, topo, core, calls):
         g.remote_dma_fused(trs, local_sem=T.sem.ls)
 
 
-def _serve(g, T, topo, core, calls, out, offs):
+def _serve(g, T, topo, core, calls, out, offs, first):
     S = T.sem
     Copy = ActivationFunctionType.Copy
     parts, b0 = [], 0
     for ci, call in enumerate(calls):
         b1 = b0 + len(call)
         bm = (b0 + b1 + 1) // 2
-        sem = S["c%d" % ci]
+        sem = S["c%d" % (first + ci)]
         g.vector.tensor_copy(out[:, CAP * b0:CAP * bm], T.tabs[:, :].indirect(offs[:, 4 * b0:4 * bm])).then_inc(sem, 1)
         if b1 > bm:
             g.scalar.activation(out[:, CAP * bm:CAP * b1], T.tabs[:, :].indirect(offs[:, 4 * bm:4 * b1]), Copy).then_inc(sem, 1)
@@ -160,6 +173,7 @@ def _serve(g, T, topo, core, calls, out, offs):
     for ci, (sem, cnt) in enumerate(parts):
         g.wait_ge(sem, cnt)
         _emit(g, T, topo, core, [calls[ci]])
+    return first + len(calls)
 
 
 def rank_program(g, core, T, topo):
@@ -176,12 +190,17 @@ def rank_program(g, core, T, topo):
                 _emit(g, T, topo, core, snd["tab%d" % i])
         g.wait_ge(S.fq, P["expect"][(core, "fq")])
         _emit(g, T, topo, core, snd["q"])
-        if "r" in snd:
+        nxt = 0
+        for q in (g.vector, g.scalar):
+            for i in range(NCH):
+                q.wait_ge(S["tb%d" % i], P["expect"][(core, "tb%d" % i)])
+        if "rs" in snd:
             for q in (g.vector, g.scalar):
-                for i in range(NCH):
-                    q.wait_ge(S["tb%d" % i], P["expect"][(core, "tb%d" % i)])
-                q.wait_ge(S.rqx, P["expect"][(core, "rqx")])
-            _serve(g, T, topo, core, snd["r"], T.gx, T.offx)
+                q.wait_ge(S.rqs, P["expect"][(core, "rqs")])
+            nxt = _serve(g, T, topo, core, snd["rs"], T.gs, T.offs, nxt)
+        for q in (g.vector, g.scalar):
+            q.wait_ge(S.rqx, P["expect"][(core, "rqx")])
+        _serve(g, T, topo, core, snd["r"], T.gx, T.offx, nxt)
         g.wait_ge(S.ls, P["local"][core])
         return
 
@@ -301,7 +320,7 @@ def rank_program(g, core, T, topo):
     g.scalar.activation(T.land[:, CAP * rank:CAP * rank + CAP], T.tabs[:, :].indirect(T.req[:, 4 * rank:4 * rank + 4]), Copy).then_inc(S.slf, 1)
     vec.wait_ge(S.rqs, P["expect"][(core, "rqs")])
     g.scalar.wait_ge(S.rqs, P["expect"][(core, "rqs")])
-    _serve(g, T, topo, core, snd["rdir"], T.gs, T.offs)
+    _serve(g, T, topo, core, snd["rdir"], T.gs, T.offs, 0)
 
     level()
     vec.wait_ge(S.sx, 16)

import numpy as np
from concourse.bass import DstId, RemoteDMATransfer
from concourse.mybir import dt, AluOpType, AxisListType, ActivationFunctionType

N = 12
RP = 4096
TT = 256
CAP = 64
NSIM = 256
NSV = 2
NCH = 4
MOST = 4

SCRATCH = {
    "idxs": ("sbuf", [128, 2], "int32"),
    "tabs": ("sbuf", [128, RP], "bfloat16"),
    "xs": ("sbuf", [128, TT], "bfloat16"),
    "ys": ("sbuf", [128, TT], "bfloat16"),
    "rowj": ("sbuf", [128, 128], "bfloat16"),
    "i16": ("sbuf", [128, 128], "bfloat16"),
    "pci": ("sbuf", [128, 1], "int32"),
    "pcf": ("sbuf", [128, 1], "float32"),
    "ones": ("sbuf", [128, 128], "bfloat16"),
    "ltri": ("sbuf", [128, 128], "bfloat16"),
    "ib": ("sbuf", [128, 6], "int32"),
    "fb": ("sbuf", [128, 6], "float32"),
    "eh": ("sbuf", [128, 32], "bfloat16"),
    "o64": ("sbuf", [128, 2], "float32"),
    "ec": ("sbuf", [128, 32], "float32"),
    "kk": ("sbuf", [128, 2], "float32"),
    "posi": ("sbuf", [128, 2], "int32"),
    "kb": ("sbuf", [128, 4], "int32"),
    "kf": ("sbuf", [128, 4], "float32"),
    "a0": ("sbuf", [128, 128], "bfloat16"),
    "a1": ("sbuf", [128, 128], "bfloat16"),
    "bb": ("sbuf", [128, 192], "bfloat16"),
    "req": ("sbuf", [128, 4 * N], "uint16"),
    "posf": ("sbuf", [128, 2], "float32"),
    "pb": ("sbuf", [128, 2], "int32"),
    "pbf": ("sbuf", [128, 2], "float32"),
    "pm": ("sbuf", [128, 128], "float32"),
    "cc": ("sbuf", [128, 2], "float32"),
    "cm": ("sbuf", [128, 32], "float32"),
    "a2": ("sbuf", [128, 128], "float32"),
    "a3": ("sbuf", [128, 128], "float32"),
    "fo": ("sbuf", [128, 16], "uint16"),
    "offs": ("sbuf", [128, 4 * N], "uint16"),
    "offx": ("sbuf", [128, 4 * N], "uint16"),
    "gs": ("sbuf", [128, CAP * N], "bfloat16"),
    "gx": ("sbuf", [128, CAP * N], "bfloat16"),
    "land": ("sbuf", [128, CAP * N], "bfloat16"),
    "rq": ("sbuf", [128, 4 * N], "uint16"),
    "ps1": ("psum", [128, 512], "float32"),
    "ps2": ("psum", [128, 512], "float32"),
    "ps3": ("psum", [128, 512], "float32"),
}
SEMAPHORES = ["sidx", "stab0", "stab1", "stab2", "stab3", "sx", "sy", "ga", "gb", "gk", "v", "p", "ls", "fq",
              "tb0", "tb1", "tb2", "tb3", "rqs", "rqx", "lnd",
              "e0", "h0", "c0", "c1", "c2", "c3", "slf"]

_memo = {}


def _engines(mask):
    return [e for e in range(16) if (mask >> e) & 1]


def _calls(items, engs):
    out, i = [], 0
    while i < len(items):
        t = 1
        while t * 2 <= min(len(items) - i, len(engs)):
            t *= 2
        w = len(engs) // t
        out.append([(sum(1 << e for e in engs[j * w:(j + 1) * w]),) + tuple(items[i + j]) for j in range(t)])
        i += t
    return out


def plan(cores, topo):
    if "p" in _memo:
        return _memo["p"]
    n = len(cores)
    same, cross, servers, per, kept, lent = [], [], [], [], [], []
    for r, c in enumerate(cores):
        ring = [(r + 1 + i) % n for i in range(n - 1)]
        same.append([s for s in ring if topo.same_plane(c, cores[s])])
        cross.append([s for s in ring if not topo.same_plane(c, cores[s])])
        cand = [d for d in range(NSIM) if d not in cores and topo.host(d) == topo.host(c) and topo.chip(d) == topo.chip(c)
                and all(topo.may_write(d, cores[s]) for s in cross[r])]
        cand.sort(key=lambda d: (topo.die(d) != topo.die(c), d))
        servers.append(cand[:NSV])
        per.append((len(cross[r]) + NSV - 1) // NSV)
        room = max(0, MOST - per[r])
        k = max(len(same[r]) - NSV * room, 0)
        kept.append(same[r][:k])
        lent.append([same[r][k + room * j:k + room * (j + 1)] for j in range(NSV)])
    sends, expect, local, role = {}, {}, {}, {}

    def add(core, phase, items, engs):
        if not items:
            return
        cs = _calls(items, engs)
        sends.setdefault(core, {})[phase] = cs
        for call in cs:
            for (mask, d, sem, s, t) in call:
                e = len(_engines(mask))
                expect[(d, sem)] = expect.get((d, sem), 0) + e
                local[core] = local.get(core, 0) + e

    def desk(s, r):
        i = cross[s].index(r)
        return servers[s][i // per[s]], i % per[s]

    def counter(s, r):
        if r in kept[s]:
            return cores[s], kept[s].index(r)
        for j in range(NSV):
            if r in lent[s][j]:
                return servers[s][j], lent[s][j].index(r)

    for r, c in enumerate(cores):
        off = _engines(topo.mask(c, cores[same[r][0]]))
        onc = _engines(topo.mask(c, servers[r][0]))
        for i in range(NCH):
            a, b = RP * i // NCH, RP * (i + 1) // NCH
            u = servers[r][i % NSV]
            add(c, "tab%d" % i, [(u, "tb%d" % i, ("tabs", a, b), ("tabs", a, b))], onc)
            add(u, "tab%d" % i, [(w, "tb%d" % i, ("tabs", a, b), ("tabs", a, b)) for w in servers[r] if w != u],
                _engines(topo.mask(u, servers[r][(i + 1) % NSV])))
        add(c, "qfeed", [(d, "fq", ("req", 0, 4 * n), ("rq", 0, 4 * n)) for d in servers[r]], onc)
        add(c, "qdir", [(counter(s, r)[0], "rqs", ("req", 4 * s, 4 * s + 4), ("offs", 4 * counter(s, r)[1], 4 * counter(s, r)[1] + 4))
                        for s in same[r]], off)
        add(c, "rdir", [(cores[s], "lnd", ("gs", CAP * i, CAP * i + CAP), ("land", CAP * r, CAP * r + CAP))
                        for i, s in enumerate(kept[r])], off)
        for j, d in enumerate(servers[r]):
            role[d] = r
            mine = cross[r][per[r] * j:per[r] * (j + 1)]
            eo = _engines(topo.mask(d, cores[mine[0]]))
            add(d, "q", [(desk(s, r)[0], "rqx", ("rq", 4 * s, 4 * s + 4), ("offx", 4 * desk(s, r)[1], 4 * desk(s, r)[1] + 4))
                         for s in mine], eo)
            add(d, "rs", [(cores[s], "lnd", ("gs", CAP * i, CAP * i + CAP), ("land", CAP * r, CAP * r + CAP))
                          for i, s in enumerate(lent[r][j])], eo)
            add(d, "r", [(cores[s], "lnd", ("gx", CAP * i, CAP * i + CAP), ("land", CAP * r, CAP * r + CAP))
                         for i, s in enumerate(mine)], eo)
    _memo["p"] = dict(sends=sends, expect=expect, local=local, role=role)
    return _memo["p"]


def _emit(g, T, topo, core, calls):
    for call in calls:
        trs = []
        for (mask, d, sem, s, t) in call:
            rid, pid = topo.addr(d, core)
            trs.append(RemoteDMATransfer(dst_ids=[DstId(rid=rid, pnc=pid)], dma_engine_mask=mask, remote_sem=T.sem[sem],
                                         src=T[s[0]][:, s[1]:s[2]], dst=T[t[0]][:, t[1]:t[2]]))
        g.remote_dma_fused(trs, local_sem=T.sem.ls)


def _serve(g, T, topo, core, calls, out, offs, first):
    S = T.sem
    Copy = ActivationFunctionType.Copy
    parts, b0 = [], 0
    for ci, call in enumerate(calls):
        b1 = b0 + len(call)
        bm = (b0 + b1 + 1) // 2
        sem = S["c%d" % (first + ci)]
        g.vector.tensor_copy(out[:, CAP * b0:CAP * bm], T.tabs[:, :].indirect(offs[:, 4 * b0:4 * bm])).then_inc(sem, 1)
        if b1 > bm:
            g.scalar.activation(out[:, CAP * bm:CAP * b1], T.tabs[:, :].indirect(offs[:, 4 * bm:4 * b1]), Copy).then_inc(sem, 1)
        parts.append((sem, 2 if b1 > bm else 1))
        b0 = b1
    for ci, (sem, cnt) in enumerate(parts):
        g.wait_ge(sem, cnt)
        _emit(g, T, topo, core, [calls[ci]])
    return first + len(calls)


def rank_program(g, core, T, topo):
    P = plan(list(T.cores), topo)
    rank = T.rank_of(core)
    S = T.sem
    if rank is None:
        if core not in P["role"]:
            return
        snd = P["sends"][core]
        for i in range(NCH):
            if "tab%d" % i in snd:
                g.wait_ge(S["tb%d" % i], P["expect"][(core, "tb%d" % i)])
                _emit(g, T, topo, core, snd["tab%d" % i])
        g.wait_ge(S.fq, P["expect"][(core, "fq")])
        _emit(g, T, topo, core, snd["q"])
        nxt = 0
        for q in (g.vector, g.scalar):
            for i in range(NCH):
                q.wait_ge(S["tb%d" % i], P["expect"][(core, "tb%d" % i)])
        if "rs" in snd:
            for q in (g.vector, g.scalar):
                q.wait_ge(S.rqs, P["expect"][(core, "rqs")])
            nxt = _serve(g, T, topo, core, snd["rs"], T.gs, T.offs, nxt)
        for q in (g.vector, g.scalar):
            q.wait_ge(S.rqx, P["expect"][(core, "rqx")])
        _serve(g, T, topo, core, snd["r"], T.gx, T.offx, nxt)
        g.wait_ge(S.ls, P["local"][core])
        return

    A = AluOpType
    Copy = ActivationFunctionType.Copy
    snd = P["sends"][core]
    nv = [0]
    vec = g.vector
    ts = vec.tensor_scalar

    def V(ins):
        ins.then_inc(S.v, 1)
        nv[0] += 1

    def level():
        vec.wait_ge(S.v, nv[0])
        return nv[0]

    g.sync.dma_start(T.idxs[:, :], T.idx[:, :]).then_inc(S.sidx, 16)
    for i in range(NCH):
        a, b = RP * i // NCH, RP * (i + 1) // NCH
        g.sync.dma_start(T.tabs[:, a:b], T.tab[:, a:b]).then_inc(S["stab%d" % i], 16)
    g.sync.dma_start(T.xs[:, :], T.x[:, :]).then_inc(S.sx, 16)

    g.iota(T.pci[:, :], [[0, 1]], 0, 1).then_inc(S.ga, 1)
    g.iota(T.rowj[:, :], [[1, 128]], 0, 0, allow_small_or_imprecise_dtypes=True).then_inc(S.gb, 1)
    g.iota(T.i16[:, :], [[0, 8], [1, 16]], 0, 0, allow_small_or_imprecise_dtypes=True).then_inc(S.gk, 1)
    for i in range(NCH):
        g.wait_ge(S["stab%d" % i], 16)
        _emit(g, T, topo, core, snd["tab%d" % i])

    V(vec.memset(T.ones[:, :], 1.0))
    vec.wait_ge(S.ga, 1)
    V(vec.tensor_copy(T.pcf[:, :], T.pci[:, :]))
    V(ts(T.pb[:, 0:1], T.pci[:, :], 3, None, A.arith_shift_right))
    V(ts(T.pb[:, 1:2], T.pci[:, :], 7, None, A.bitwise_and))
    level()
    vec.wait_ge(S.gb, 1)
    V(ts(T.ltri[:, :], T.rowj[:, :], T.pcf[:, 0:1], None, A.is_gt))
    V(vec.tensor_copy(T.pbf[:, :], T.pb[:, :]))

    vec.wait_ge(S.sidx, 16)
    V(ts(T.ib[:, 0:2], T.idxs[:, :], 12, None, A.arith_shift_right))
    level()
    V(vec.tensor_copy(T.fb[:, 0:2], T.ib[:, 0:2]))
    consts = level()
    ts(T.eh[:, 0:16], T.rowj[:, 0:16], T.fb[:, 0:1], None, A.is_equal).then_inc(S.e0, 1)
    V(ts(T.eh[:, 16:32], T.rowj[:, 0:16], T.fb[:, 1:2], None, A.is_equal))
    g.tensor.wait_ge(S.v, consts)
    g.tensor.wait_ge(S.e0, 1)
    g.tensor.matmul(T.ps1[:, 0:16], T.ltri[:, :], T.eh[:, 0:16], True, True).then_inc(S.p, 1)
    g.tensor.matmul(T.ps1[:, 16:32], T.ones[:, :], T.eh[:, 0:16], True, False)
    g.tensor.wait_ge(S.v, level())
    g.tensor.matmul(T.ps1[:, 16:32], T.ltri[:, :], T.eh[:, 16:32], False, True).then_inc(S.p, 1)
    vec.wait_ge(S.e0, 1)
    V(ts(T.ib[:, 2:4], T.idxs[:, :], RP - CAP, None, A.bitwise_and))
    V(ts(T.ib[:, 4:6], T.idxs[:, :], CAP - 1, None, A.bitwise_and))
    V(ts(T.o64[:, :], T.fb[:, 0:2], float(CAP), None, A.mult))
    level()
    V(vec.tensor_copy(T.fb[:, 2:6], T.ib[:, 2:6]))
    vec.wait_ge(S.p, 2)
    V(vec.tensor_tensor(T.ec[:, :], T.eh[:, :], T.ps1[:, 0:32], A.mult))
    level()
    V(vec.tensor_reduce(T.kk[:, 0:1], T.ec[:, 0:16], AxisListType.X, A.add))
    V(vec.tensor_reduce(T.kk[:, 1:2], T.ec[:, 16:32], AxisListType.X, A.add))
    level()
    V(vec.tensor_tensor(T.posi[:, :], T.kk[:, :], T.o64[:, :], A.add))
    level()
    V(ts(T.kb[:, 0:2], T.posi[:, :], 4, None, A.arith_shift_right))
    V(ts(T.kb[:, 2:4], T.posi[:, :], 15, None, A.bitwise_and))
    level()
    V(vec.tensor_copy(T.kf[:, :], T.kb[:, :]))
    level()
    vec.wait_ge(S.gk, 1)
    for h, ah in enumerate((T.a0, T.a1)):
        ins = [ts(ah[:, :], T.i16[:, :], T.kf[:, 2 + h:3 + h], None, A.is_equal),
               ts(T.bb[:, 96 * h:96 * h + 48], T.rowj[:, 0:48], T.kf[:, h:h + 1], T.fb[:, 2 + h:3 + h], A.is_equal, A.mult),
               ts(T.bb[:, 96 * h + 48:96 * h + 96], T.rowj[:, 0:48], T.kf[:, h:h + 1], T.fb[:, 4 + h:5 + h], A.is_equal, A.mult)]
        for i in ins:
            if h == 0:
                i.then_inc(S.h0, 1)
            else:
                V(i)
    g.tensor.wait_ge(S.h0, 3)
    g.tensor.matmul(T.ps2[:, 0:48], T.a0[:, :], T.bb[:, 0:48], True, False)
    g.tensor.matmul(T.ps2[:, 0:48], T.a0[:, :], T.bb[:, 48:96], False, False)
    g.tensor.wait_ge(S.v, level())
    g.tensor.matmul(T.ps2[:, 0:48], T.a1[:, :], T.bb[:, 96:144], False, False)
    g.tensor.matmul(T.ps2[:, 0:48], T.a1[:, :], T.bb[:, 144:192], False, True).then_inc(S.p, 1)
    V(vec.tensor_tensor(T.posf[:, :], T.kk[:, :], T.o64[:, :], A.add))
    vec.wait_ge(S.p, 3)
    V(vec.tensor_copy(T.req[:, :], T.ps2[:, 0:48]))

    req_done = level()
    g.wait_ge(S.v, req_done)
    _emit(g, T, topo, core, snd["qfeed"])
    _emit(g, T, topo, core, snd["qdir"])

    V(ts(T.pm[:, :], T.i16[:, :], T.pbf[:, 0:1], None, A.is_equal))
    for h in range(2):
        V(ts(T.cc[:, h:h + 1], T.pbf[:, 1:2], 2.0, float(h), A.mult, A.add))
    level()
    for h in range(2):
        V(ts(T.cm[:, 16 * h:16 * h + 16], T.rowj[:, 0:16], T.cc[:, h:h + 1], None, A.is_equal))
    V(ts(T.a2[:, :], T.pm[:, :], T.posf[:, 0:1], None, A.mult))
    V(ts(T.a3[:, :], T.pm[:, :], T.posf[:, 1:2], None, A.mult))
    g.tensor.wait_ge(S.v, level())
    g.tensor.matmul(T.ps3[:, 0:16], T.a2[:, :], T.cm[:, 0:16], True, False)
    g.tensor.matmul(T.ps3[:, 0:16], T.a3[:, :], T.cm[:, 16:32], False, True).then_inc(S.p, 1)
    vec.wait_ge(S.p, 4)
    V(vec.tensor_copy(T.fo[:, :], T.ps3[:, 0:16]))

    g.scalar.wait_ge(S.v, req_done)
    for i in range(NCH):
        g.scalar.wait_ge(S["stab%d" % i], 16)
        vec.wait_ge(S["stab%d" % i], 16)
    g.scalar.activation(T.land[:, CAP * rank:CAP * rank + CAP], T.tabs[:, :].indirect(T.req[:, 4 * rank:4 * rank + 4]), Copy).then_inc(S.slf, 1)
    vec.wait_ge(S.rqs, P["expect"][(core, "rqs")])
    g.scalar.wait_ge(S.rqs, P["expect"][(core, "rqs")])
    _serve(g, T, topo, core, snd["rdir"], T.gs, T.offs, 0)

    level()
    vec.wait_ge(S.sx, 16)
    vec.wait_ge(S.slf, 1)
    vec.wait_ge(S.lnd, P["expect"][(core, "lnd")])
    V(vec.tensor_tensor(T.ys[:, :], T.land[:, :].indirect(T.fo[:, :]), T.xs[:, :], A.add))
    g.sync.wait_ge(S.v, level())
    g.sync.dma_start(T.y[:, :], T.ys[:, :]).then_inc(S.sy, 16)
    g.sync.wait_ge(S.sy, 16)
    g.wait_ge(S.ls, P["local"][core])
